import numpy as np
import ml_dtypes

BF16 = ml_dtypes.bfloat16


def bf(x):
    return np.asarray(x, np.float32).astype(BF16)


def f32(x):
    return np.asarray(x, np.float32)


def f64(x):
    return np.asarray(x).astype(np.float64)


def striped(idx):
    return np.concatenate([l.reshape(-1, 16).T for l in idx])


def rows(idx, k):
    return np.tile(np.repeat(idx, 16, axis=0), (k // (16 * 8), 1))


def look(tab, idx):
    return np.take_along_axis(f64(tab), rows(idx, len(tab)), axis=1)


K, S, D, V, N, M = 512, 2048, 4, 512, 2048, 256


def setup_inputs():
    return {"tab": f32(np.random.standard_normal((K, S))), "x0": f32(np.random.standard_normal((K, V))), "w": bf(np.random.standard_normal((K, M)) / np.sqrt(K)), "offs": striped(np.stack([np.random.permutation(S)[:N] for _ in range(8)]))}


def reference(tab, x0, w, offs):
    idx = np.stack([g.T.reshape(-1) for g in np.split(offs, 8)])
    x = f64(x0)
    for d in range(D):
        x = np.minimum(x, look(tab, idx[:, d * V:(d + 1) * V]))
    y = f64(w).T @ x
    return y

@@ -1,0 +1,64 @@
+import concourse.mybir as mybir
+
+P = 128
+ROWS, COLS = 512, 2048
+STEPS, WIDTH = 4, 512
+HIDDEN = 256
+BLOCKS = ROWS // P
+LISTED = WIDTH // 16
+
+F32, BF16, U16 = mybir.dt.float32, mybir.dt.bfloat16, mybir.dt.uint16
+FLOPS = 2 * ROWS * HIDDEN * WIDTH
+
+
+def tile_lookup_pool_min_none_kernel(tc, tab, x0, w, offs, out):
+    nc = tc.nc
+    with (
+        tc.tile_pool(name="held", bufs=1) as held,
+        tc.tile_pool(name="ring", bufs=2) as ring,
+        tc.psum_pool(name="psum", bufs=1) as psum,
+    ):
+        offsets = held.tile([P, STEPS * LISTED], U16, name="offsets")
+        nc.sync.dma_start(offsets[:], offs)
+
+        centres, windows = [], []
+        for b in range(BLOCKS):
+            rows = slice(b * P, (b + 1) * P)
+            centre = held.tile([P, WIDTH], F32, name=f"centre{b}")
+            nc.sync.dma_start(centre[:], x0[rows, :])
+            window = held.tile([P, COLS], F32, name=f"window{b}")
+            nc.sync.dma_start(window[:], tab[rows, :])
+            centres.append(centre)
+            windows.append(window)
+        weights = held.tile([P, BLOCKS, HIDDEN], BF16, name="weights")
+        nc.scalar.dma_start(weights[:], w.rearrange("(b p) m -> p b m", p=P))
+
+        sums = [psum.tile([P, WIDTH], F32, name=f"sums{h}") for h in range(HIDDEN // P)]
+        for b in range(BLOCKS):
+            x = centres[b]
+            for d in range(STEPS):
+                smaller = ring.tile([P, WIDTH], F32, name="smaller")
+                nc.vector.tensor_tensor(
+                    smaller[:],
+                    windows[b][:].indirect(offsets[:, d * LISTED : (d + 1) * LISTED]),
+                    x[:],
+                    mybir.AluOpType.min,
+                )
+                x = smaller
+            rounded = ring.tile([P, WIDTH], BF16, name="rounded")
+            nc.scalar.copy(rounded[:], x[:])
+            for h in range(HIDDEN // P):
+                nc.tensor.matmul(
+                    sums[h][:],
+                    weights[:, b, h * P : (h + 1) * P],
+                    rounded[:],
+                    start=b == 0,
+                    stop=b == BLOCKS - 1,
+                )
+
+        result0 = held.tile([P, WIDTH], F32, name="result0")
+        nc.vector.tensor_copy(result0[:], sums[0][:])
+        nc.sync.dma_start(out[0:P, :], result0[:])
+        result1 = held.tile([P, WIDTH], F32, name="result1")
+        nc.scalar.copy(result1[:], sums[1][:])
+        nc.scalar.dma_start(out[P : 2 * P, :], result1[:])

@@ -6,6 +6,7 @@ STEPS, WIDTH = 4, 512
 HIDDEN = 256
 BLOCKS = ROWS // P
 LISTED = WIDTH // 16
+LAG = 2
 
 F32, BF16, U16 = mybir.dt.float32, mybir.dt.bfloat16, mybir.dt.uint16
 FLOPS = 2 * ROWS * HIDDEN * WIDTH
@@ -15,7 +16,7 @@ def tile_lookup_pool_min_none_kernel(tc, tab, x0, w, offs, out):
     nc = tc.nc
     with (
         tc.tile_pool(name="held", bufs=1) as held,
-        tc.tile_pool(name="ring", bufs=2) as ring,
+        tc.tile_pool(name="ring", bufs=4) as ring,
         tc.psum_pool(name="psum", bufs=1) as psum,
     ):
         offsets = held.tile([P, STEPS * LISTED], U16, name="offsets")
@@ -34,27 +35,33 @@ def tile_lookup_pool_min_none_kernel(tc, tab, x0, w, offs, out):
         nc.scalar.dma_start(weights[:], w.rearrange("(b p) m -> p b m", p=P))
 
         sums = [psum.tile([P, WIDTH], F32, name=f"sums{h}") for h in range(HIDDEN // P)]
-        for b in range(BLOCKS):
-            x = centres[b]
-            for d in range(STEPS):
+
+        x = list(centres)
+        for step in range(STEPS + LAG * (BLOCKS - 1)):
+            for b in range(BLOCKS):
+                d = step - LAG * b
+                if not 0 <= d < STEPS:
+                    continue
                 smaller = ring.tile([P, WIDTH], F32, name="smaller")
                 nc.vector.tensor_tensor(
                     smaller[:],
                     windows[b][:].indirect(offsets[:, d * LISTED : (d + 1) * LISTED]),
-                    x[:],
+                    x[b][:],
                     mybir.AluOpType.min,
                 )
-                x = smaller
-            rounded = ring.tile([P, WIDTH], BF16, name="rounded")
-            nc.scalar.copy(rounded[:], x[:])
-            for h in range(HIDDEN // P):
-                nc.tensor.matmul(
-                    sums[h][:],
-                    weights[:, b, h * P : (h + 1) * P],
-                    rounded[:],
-                    start=b == 0,
-                    stop=b == BLOCKS - 1,
-                )
+                x[b] = smaller
+                if d < STEPS - 1:
+                    continue
+                rounded = ring.tile([P, WIDTH], BF16, name="rounded")
+                nc.scalar.copy(rounded[:], x[b][:])
+                for h in range(HIDDEN // P):
+                    nc.tensor.matmul(
+                        sums[h][:],
+                        weights[:, b, h * P : (h + 1) * P],
+                        rounded[:],
+                        start=b == 0,
+                        stop=b == BLOCKS - 1,
+                    )
 
         result0 = held.tile([P, WIDTH], F32, name="result0")
         nc.vector.tensor_copy(result0[:], sums[0][:])

@@ -22,6 +22,7 @@ def tile_lookup_pool_min_none_kernel(tc, tab, x0, w, offs, out):
         offsets = held.tile([P, STEPS * LISTED], U16, name="offsets")
         nc.sync.dma_start(offsets[:], offs)
 
+        weights = held.tile([P, BLOCKS, HIDDEN], BF16, name="weights")
         centres, windows = [], []
         for b in range(BLOCKS):
             rows = slice(b * P, (b + 1) * P)
@@ -31,17 +32,19 @@ def tile_lookup_pool_min_none_kernel(tc, tab, x0, w, offs, out):
             nc.sync.dma_start(window[:], tab[rows, :])
             centres.append(centre)
             windows.append(window)
-        weights = held.tile([P, BLOCKS, HIDDEN], BF16, name="weights")
-        nc.scalar.dma_start(weights[:], w.rearrange("(b p) m -> p b m", p=P))
+            if b == 1:
+                nc.sync.dma_start(weights[:], w.rearrange("(b p) m -> p b m", p=P))
 
-        sums = [psum.tile([P, WIDTH], F32, name=f"sums{h}") for h in range(HIDDEN // P)]
+        halves = [slice(0, WIDTH // 2), slice(WIDTH // 2, WIDTH)]
+        sums = [[psum.tile([P, WIDTH // 2], F32, name=f"sums{h}{c}") for c in range(2)] for h in range(HIDDEN // P)]
 
         x = list(centres)
-        for step in range(STEPS + LAG * (BLOCKS - 1)):
-            for b in range(BLOCKS):
-                d = step - LAG * b
-                if not 0 <= d < STEPS:
+        for turn in range(STEPS * BLOCKS // 2 + LAG):
+            for lane in range(2):
+                step = turn - LAG * lane
+                if not 0 <= step < STEPS * BLOCKS // 2:
                     continue
+                b, d = 2 * (step // STEPS) + lane, step % STEPS
                 smaller = ring.tile([P, WIDTH], F32, name="smaller")
                 nc.vector.tensor_tensor(
                     smaller[:],
@@ -52,20 +55,25 @@ def tile_lookup_pool_min_none_kernel(tc, tab, x0, w, offs, out):
                 x[b] = smaller
                 if d < STEPS - 1:
                     continue
-                rounded = ring.tile([P, WIDTH], BF16, name="rounded")
-                nc.scalar.copy(rounded[:], x[b][:])
-                for h in range(HIDDEN // P):
-                    nc.tensor.matmul(
-                        sums[h][:],
-                        weights[:, b, h * P : (h + 1) * P],
-                        rounded[:],
-                        start=b == 0,
-                        stop=b == BLOCKS - 1,
-                    )
+                for c, columns in enumerate(halves):
+                    rounded = ring.tile([P, WIDTH // 2], BF16, name=f"rounded{c}")
+                    if b < BLOCKS - 1:
+                        nc.scalar.copy(rounded[:], x[b][:, columns])
+                    else:
+                        nc.vector.tensor_copy(rounded[:], x[b][:, columns])
+                    for h in range(HIDDEN // P):
+                        nc.tensor.matmul(
+                            sums[h][c][:],
+                            weights[:, b, h * P : (h + 1) * P],
+                            rounded[:],
+                            start=b == 0,
+                            stop=b == BLOCKS - 1,
+                        )
 
-        result0 = held.tile([P, WIDTH], F32, name="result0")
-        nc.vector.tensor_copy(result0[:], sums[0][:])
-        nc.sync.dma_start(out[0:P, :], result0[:])
-        result1 = held.tile([P, WIDTH], F32, name="result1")
-        nc.scalar.copy(result1[:], sums[1][:])
-        nc.scalar.dma_start(out[P : 2 * P, :], result1[:])
+        for c, columns in enumerate(halves):
+            upper = held.tile([P, WIDTH // 2], F32, name=f"upper{c}")
+            nc.vector.tensor_copy(upper[:], sums[0][c][:])
+            nc.sync.dma_start(out[0:P, columns], upper[:])
+            lower = held.tile([P, WIDTH // 2], F32, name=f"lower{c}")
+            nc.scalar.copy(lower[:], sums[1][c][:])
+            nc.sync.dma_start(out[P : 2 * P, columns], lower[:])

@@ -6,7 +6,6 @@ STEPS, WIDTH = 4, 512
 HIDDEN = 256
 BLOCKS = ROWS // P
 LISTED = WIDTH // 16
-LAG = 2
 
 F32, BF16, U16 = mybir.dt.float32, mybir.dt.bfloat16, mybir.dt.uint16
 FLOPS = 2 * ROWS * HIDDEN * WIDTH
@@ -38,13 +37,13 @@ def tile_lookup_pool_min_none_kernel(tc, tab, x0, w, offs, out):
         halves = [slice(0, WIDTH // 2), slice(WIDTH // 2, WIDTH)]
         sums = [[psum.tile([P, WIDTH // 2], F32, name=f"sums{h}{c}") for c in range(2)] for h in range(HIDDEN // P)]
 
+        first_turn = {0: 0, 2: STEPS, 1: 1, 3: STEPS}
         x = list(centres)
-        for turn in range(STEPS * BLOCKS // 2 + LAG):
-            for lane in range(2):
-                step = turn - LAG * lane
-                if not 0 <= step < STEPS * BLOCKS // 2:
+        for turn in range(2 * STEPS):
+            for b, start in first_turn.items():
+                d = turn - start
+                if not 0 <= d < STEPS:
                     continue
-                b, d = 2 * (step // STEPS) + lane, step % STEPS
                 smaller = ring.tile([P, WIDTH], F32, name="smaller")
                 nc.vector.tensor_tensor(
                     smaller[:],

import concourse.mybir as mybir

P = 128
ROWS, COLS = 512, 2048
STEPS, WIDTH = 4, 512
HIDDEN = 256
BLOCKS = ROWS // P
LISTED = WIDTH // 16

F32, BF16, U16 = mybir.dt.float32, mybir.dt.bfloat16, mybir.dt.uint16
FLOPS = 2 * ROWS * HIDDEN * WIDTH


def tile_lookup_pool_min_none_kernel(tc, tab, x0, w, offs, out):
    nc = tc.nc
    with (
        tc.tile_pool(name="held", bufs=1) as held,
        tc.tile_pool(name="ring", bufs=4) as ring,
        tc.psum_pool(name="psum", bufs=1) as psum,
    ):
        offsets = held.tile([P, STEPS * LISTED], U16, name="offsets")
        nc.sync.dma_start(offsets[:], offs)

        weights = held.tile([P, BLOCKS, HIDDEN], BF16, name="weights")
        centres, windows = [], []
        for b in range(BLOCKS):
            rows = slice(b * P, (b + 1) * P)
            centre = held.tile([P, WIDTH], F32, name=f"centre{b}")
            nc.sync.dma_start(centre[:], x0[rows, :])
            window = held.tile([P, COLS], F32, name=f"window{b}")
            nc.sync.dma_start(window[:], tab[rows, :])
            centres.append(centre)
            windows.append(window)
            if b == 1:
                nc.sync.dma_start(weights[:], w.rearrange("(b p) m -> p b m", p=P))

        halves = [slice(0, WIDTH // 2), slice(WIDTH // 2, WIDTH)]
        sums = [[psum.tile([P, WIDTH // 2], F32, name=f"sums{h}{c}") for c in range(2)] for h in range(HIDDEN // P)]

        first_turn = {0: 0, 2: STEPS, 1: 1, 3: STEPS}
        x = list(centres)
        for turn in range(2 * STEPS):
            for b, start in first_turn.items():
                d = turn - start
                if not 0 <= d < STEPS:
                    continue
                smaller = ring.tile([P, WIDTH], F32, name="smaller")
                nc.vector.tensor_tensor(
                    smaller[:],
                    windows[b][:].indirect(offsets[:, d * LISTED : (d + 1) * LISTED]),
                    x[b][:],
                    mybir.AluOpType.min,
                )
                x[b] = smaller
                if d < STEPS - 1:
                    continue
                for c, columns in enumerate(halves):
                    rounded = ring.tile([P, WIDTH // 2], BF16, name=f"rounded{c}")
                    if b < BLOCKS - 1:
                        nc.scalar.copy(rounded[:], x[b][:, columns])
                    else:
                        nc.vector.tensor_copy(rounded[:], x[b][:, columns])
                    for h in range(HIDDEN // P):
                        nc.tensor.matmul(
                            sums[h][c][:],
                            weights[:, b, h * P : (h + 1) * P],
                            rounded[:],
                            start=b == 0,
                            stop=b == BLOCKS - 1,
                        )

        for c, columns in enumerate(halves):
            upper = held.tile([P, WIDTH // 2], F32, name=f"upper{c}")
            nc.vector.tensor_copy(upper[:], sums[0][c][:])
            nc.sync.dma_start(out[0:P, columns], upper[:])
            lower = held.tile([P, WIDTH // 2], F32, name=f"lower{c}")
            nc.scalar.copy(lower[:], sums[1][c][:])
            nc.sync.dma_start(out[P : 2 * P, columns], lower[:])
